import numpy as np
import ml_dtypes


def mxq(x, axis, fmt="e4m3"):
    dtype, down = {"e4m3": (ml_dtypes.float8_e4m3fn, 7), "e5m2": (ml_dtypes.float8_e5m2, 14)}[fmt]
    v = np.moveaxis(np.asarray(x, np.float32).astype(ml_dtypes.bfloat16).astype(np.float64), axis, -1)
    blocks = v.reshape(v.shape[:-1] + (-1, 32))
    amax = np.abs(blocks).max(-1, keepdims=True)
    byte = np.maximum(np.where(amax > 0, np.frexp(amax)[1] - 1 + 127, 0) - down, 1)
    scale = np.exp2(byte - 127.0)
    codes = (blocks / scale).astype(np.float32).astype(dtype).astype(np.float64)
    return np.moveaxis((codes * scale).reshape(v.shape), -1, axis)


WIDE = False


def mx_kscale(k):
    if not WIDE:
        return np.ones(k)
    levels = np.array([10, -10, 5, -5, 0])
    if k % 512:
        return np.exp2(np.random.permutation(np.resize(levels, k // 32))).repeat(32)
    a = np.empty((k // 512, 16))
    for p in range(k // 512):
        a[p, :8] = np.random.permutation(np.resize(levels, 8))
        for g in range(8):
            far = levels[np.abs(levels - a[p, g]) >= 10]
            a[p, g + 8] = far[np.random.randint(len(far))]
    return np.exp2(a.ravel()).repeat(32)


BF16 = ml_dtypes.bfloat16


def bf(x):
    return np.asarray(x, np.float32).astype(BF16)


def f64(x):
    return np.asarray(x).astype(np.float64)


E2M1 = np.array([0.0, 0.5, 1.0, 1.5, 2.0, 3.0, 4.0, 6.0, -0.0, -0.5, -1.0, -1.5, -2.0, -3.0, -4.0, -6.0])


def pack_weight(w, fmt):
    k, n = w.shape
    w = f64(bf(w)).reshape(k // 32, 32, n)
    amax = np.abs(w).max(1)
    if fmt == "e4m3":
        byte = np.frexp(amax)[1] - 1 + 127 - 7
    else:
        mant, ex = np.frexp(amax / 6.0)
        byte = np.where(mant > 0.5, ex, ex - 1) + 127
    byte = np.clip(np.where(amax > 0, byte, 1), 1, 254)
    scaled = (w * np.exp2(127.0 - byte)[:, None, :]).reshape(k, n).astype(np.float32)
    by_word = np.ascontiguousarray(scaled.reshape(k // 512, 128, 4, n).transpose(0, 1, 3, 2))
    if fmt == "e4m3":
        words = by_word.astype(ml_dtypes.float8_e4m3fn).view(np.uint8)
    else:
        c = by_word.astype(ml_dtypes.float4_e2m1fn).view(np.uint8) & 0xF
        words = c[..., 0::2] | (c[..., 1::2] << 4)
    return np.ascontiguousarray(words), np.ascontiguousarray(byte.astype(np.uint8).reshape(k // 512, 16, n))


def unpack_weight(words, scales, fmt):
    g, p, n, _ = words.shape
    if fmt == "e4m3":
        vals = np.ascontiguousarray(words).view(ml_dtypes.float8_e4m3fn).astype(np.float64)
    else:
        nib = np.empty((g, p, n, 4), np.uint8)
        nib[..., 0::2] = words & 0xF
        nib[..., 1::2] = words >> 4
        vals = E2M1[nib]
    vals = vals * np.repeat(np.exp2(scales.astype(np.float64) - 127.0), 8, axis=1)[..., None]
    return vals.transpose(0, 1, 3, 2).reshape(g * 512, n)
def pack4(w):
    words, scales = pack_weight(w, "e2m1")
    return words.reshape(words.shape[0], 128, -1), scales


def unpack4(words, scales):
    return unpack_weight(words.reshape(words.shape[0], 128, -1, 2), scales, "e2m1")


M, K, N = 2048, 1024, 512


def sigmoid(x):
    return 1.0 / (1.0 + np.exp(-x))


def setup_inputs():
    s, t = mx_kscale(K), mx_kscale(M)
    x = np.random.standard_normal((K, M)) * s[:, None]
    wm = np.random.standard_normal((K, N)) / np.sqrt(K) / s[:, None]
    wg = np.random.standard_normal((K, N)) / np.sqrt(K) / s[:, None]
    a = np.abs(np.random.standard_normal((M, M))) / np.sqrt(M) / t[:, None]
    x_words, x_scales = pack4(x)
    wm_words, wm_scales = pack4(wm)
    wg_words, wg_scales = pack4(wg)
    a_words, a_scales = pack4(a)
    return {"x_words": x_words, "x_scales": x_scales,
            "wm_words": wm_words, "wm_scales": wm_scales,
            "wg_words": wg_words, "wg_scales": wg_scales,
            "a_words": a_words, "a_scales": a_scales,
            "bg": bf(0.5 * np.random.standard_normal(N)),
            "src": bf((0.6 + 0.8 * np.random.random(M)) * t),
            "dst": bf(0.6 + 0.8 * np.random.random(M)),
            "b": bf(0.3 * np.random.standard_normal(N))}


def reference(x_words, x_scales, wm_words, wm_scales, wg_words, wg_scales, a_words, a_scales, bg, src, dst, b):
    x = unpack4(x_words, x_scales)
    wm = unpack4(wm_words, wm_scales)
    wg = unpack4(wg_words, wg_scales)
    a = unpack4(a_words, a_scales)
    h = x.T @ wm
    z = sigmoid((x.T @ wg) + f64(bg))
    v = f64(src)[:, None] * (z * h)
    agg = a.T @ mxq(v, 0, "e4m3")
    y = f64(dst)[:, None] * agg + (1.0 - z) * h + f64(b)
    return y * sigmoid(y)

@@ -1,0 +1,235 @@
+from contextlib import ExitStack
+
+import concourse.mybir as mybir
+from concourse.masks import make_identity
+
+M, K, N = 2048, 1024, 512
+FLOPS = 2 * (2 * M * K * N) + 2 * M * M * N
+
+F32 = mybir.dt.float32
+BF16 = mybir.dt.bfloat16
+I32 = mybir.dt.int32
+U32 = mybir.dt.uint32
+U8 = mybir.dt.uint8
+FP4X4 = mybir.dt.float4_e2m1fn_x4
+FP8X4 = mybir.dt.float8_e4m3fn_x4
+ALU = mybir.AluOpType
+ACT = mybir.ActivationFunctionType
+
+P = 128
+PACK = 4
+K_PASS = P * PACK
+KG = K // K_PASS
+MG = M // K_PASS
+TILES = M // P
+BANKS = 8
+
+
+def tile_send_keep_graph_convolution_f2_kernel(
+    tc, x_words, x_scales, wm_words, wm_scales, wg_words, wg_scales, a_words, a_scales, bg, src, dst, b, out
+):
+    nc = tc.nc
+    with ExitStack() as ctx:
+        keep = ctx.enter_context(tc.tile_pool(name="keep", bufs=1))
+        work = ctx.enter_context(tc.tile_pool(name="work", bufs=3))
+        psum = ctx.enter_context(tc.psum_pool(name="psum", bufs=1))
+        ctx.enter_context(tc.manual_schedule())
+
+        def bank(i):
+            return psum.tile([P, N], F32, name="bank%d" % i, tag="bank%d" % i)
+
+        def plane(name, groups, width):
+            t = keep.tile([P, groups, width], U8, name=name, align_bytes=64)
+            nc.vector.memset(t[:].bitcast(I32), 0)
+            return t
+
+        def load_scales(t, scales):
+            for q in range(4):
+                nc.sync.dma_start(
+                    out=t[32 * q : 32 * q + 4, :, :].bitcast(I32),
+                    in_=scales.bitcast(I32)[:, 4 * q : 4 * q + 4, :].rearrange("g r n -> r g n"),
+                )
+
+        def load_words(name, words):
+            groups, width = words.shape[0], words.shape[2]
+            t = keep.tile([P, groups, width], U8, name=name, align_bytes=64)
+            nc.sync.dma_start(out=t[:].bitcast(I32), in_=words.bitcast(I32).rearrange("g p n -> p g n"))
+            return t
+
+        rows = keep.tile([P, N + P + 16], BF16, name="rows")
+        nc.vector.memset(rows[:].bitcast(I32), 0)
+        wg_s = plane("wg_s", KG, N)
+        x_s = plane("x_s", KG, M)
+        wm_s = plane("wm_s", KG, N)
+        a_s = plane("a_s", MG, M)
+
+        warm = keep.tile([P, 2], F32, name="warm")
+        nc.scalar.activation(out=warm[:, 0:1], in_=rows[:, N + P : N + P + 1], func=ACT.Sigmoid)
+
+        ident = keep.tile([P, P], BF16, name="ident")
+        make_identity(nc, ident[:])
+        nc.gpsimd.dma_start(out=rows[0:TILES, N : N + P], in_=src.rearrange("(j p) -> j p", p=P))
+        nc.gpsimd.dma_start(out=rows[TILES : 2 * TILES, N : N + P], in_=dst.rearrange("(j p) -> j p", p=P))
+
+        def x_chunk(g):
+            return load_words("x_w%d" % g, x_words[:, :, 2 * K_PASS * g : 2 * K_PASS * (g + 1)])
+
+        wg_w = load_words("wg_w", wg_words)
+        x_w = [x_chunk(0)]
+        nc.sync.dma_start(out=rows[0:1, 0:N], in_=bg.unsqueeze(0))
+        load_scales(wg_s, wg_scales)
+        load_scales(x_s, x_scales)
+        load_scales(wm_s, wm_scales)
+        wm_w = load_words("wm_w", wm_words)
+        nc.sync.dma_start(out=rows[1:2, 0:N], in_=b.unsqueeze(0))
+        for g in range(1, MG):
+            x_w.append(x_chunk(g))
+        a_w = []
+
+        def spread_row(r, name, bank_id):
+            ps = bank(bank_id)
+            nc.tensor.matmul(out=ps[:], lhsT=ident[:, r : r + 1].to_broadcast([P, P]), rhs=rows[:, 0:N], start=True, stop=True)
+            t = keep.tile([P, N], F32, name=name)
+            nc.scalar.copy(out=t[:], in_=ps[:])
+            return t
+
+        def project(j, w, w_s, bank_id):
+            ps = bank(bank_id)
+            g, jj = divmod(j, PACK)
+            for c in range(KG):
+                nc.tensor.matmul_mx(
+                    out=ps[:],
+                    lhsT=x_w[g][:, c, 2 * P * jj : 2 * P * (jj + 1)].bitcast(FP4X4),
+                    lhsT_scale=x_s[:, c, P * j : P * (j + 1)],
+                    rhs=w[:, c, :].bitcast(FP4X4),
+                    rhs_scale=w_s[:, c, :],
+                    start=(c == 0),
+                    stop=(c == KG - 1),
+                )
+            return ps
+
+        gate_ps, h_ps, z, kept, v_rows, v_il, v_codes, v_scales, agg = {}, {}, {}, {}, {}, {}, {}, {}, {}
+
+        def gate_matmul(j):
+            gate_ps[j] = project(j, wg_w, wg_s, j % 2)
+
+        def h_matmul(j):
+            h_ps[j] = project(j, wm_w, wm_s, 2 + j % 2)
+
+        def gate(j):
+            gb = work.tile([P, N], F32, name="gb")
+            nc.vector.tensor_tensor(out=gb[:], in0=gate_ps[j][:], in1=bg_all[:], op=ALU.add)
+            z[j] = work.tile([P, N], F32, name="z")
+            nc.scalar.activation(out=z[j][:], in_=gb[:], func=ACT.Sigmoid)
+
+        def message(j):
+            v = work.tile([P, N], BF16, name="v", bufs=5)
+            nc.vector.scalar_tensor_tensor(
+                out=v[:], in0=h_ps[j][:], scalar=node_f[:, j : j + 1], in1=z[j][:], op0=ALU.mult, op1=ALU.mult
+            )
+            g, jj = divmod(j, PACK)
+            if jj == 0:
+                v_rows[g] = work.tile([P, PACK, N], BF16, name="v_rows", bufs=2)
+            for t in range(PACK):
+                nc.sync.dma_start(out=v_rows[g][32 * jj : 32 * (jj + 1), t, :], in_=v[t:P:PACK, :])
+
+        def keep_part(j):
+            u = work.tile([P, N], F32, name="u")
+            nc.vector.scalar_tensor_tensor(
+                out=u[:], in0=z[j][:], scalar=1.0, in1=h_ps[j][:], op0=ALU.subtract, op1=ALU.mult
+            )
+            kept[j] = keep.tile([P, N], F32, name="kept%d" % j)
+            nc.gpsimd.tensor_tensor(out=kept[j][:], in0=b_all[:], in1=u[:], op=ALU.subtract)
+
+        def interleave(g, c0, c1, on_vector):
+            if g not in v_il:
+                v_il[g] = work.tile([P, N * PACK], BF16, name="v_il", bufs=2, align_bytes=64)
+            o = v_il[g][:, PACK * c0 : PACK * c1].rearrange("p (c i t) -> p c t i", i=4, t=PACK)
+            i = v_rows[g][:, :, c0:c1].rearrange("p t (c i) -> p c t i", i=4)
+            if on_vector:
+                nc.vector.tensor_copy(out=o, in_=i)
+            else:
+                nc.scalar.copy(out=o, in_=i)
+
+        def quantize(g):
+            v_codes[g] = keep.tile([P, N], U32, name="v_codes%d" % g, align_bytes=64)
+            v_scales[g] = keep.tile([P, N], U8, name="v_scales%d" % g, align_bytes=64)
+            nc.vector.quantize_mx(out=v_codes[g][:].bitcast(FP8X4), scales=v_scales[g][:], in_=v_il[g][:])
+
+        def mix(d, g):
+            if g == 0:
+                agg[d] = bank((d + 4) % BANKS)
+            nc.tensor.matmul_mx(
+                out=agg[d][:],
+                lhsT=a_w[g][:, 0, 2 * P * d : 2 * P * (d + 1)].bitcast(FP4X4),
+                lhsT_scale=a_s[:, g, P * d : P * (d + 1)],
+                rhs=v_codes[g][:].bitcast(FP8X4),
+                rhs_scale=v_scales[g][:],
+                start=(g == 0),
+                stop=(g == MG - 1),
+            )
+
+        def finish(d, parts=1):
+            y = work.tile([P, N], F32, name="y")
+            o = work.tile([P, N], F32, name="o", bufs=6)
+            for h in range(parts):
+                cols = slice(h * N // parts, (h + 1) * N // parts)
+                nc.vector.scalar_tensor_tensor(
+                    out=y[:, cols], in0=agg[d][:, cols], scalar=node_f[:, TILES + d : TILES + d + 1],
+                    in1=kept[d][:, cols], op0=ALU.mult, op1=ALU.add,
+                )
+                nc.scalar.activation(out=o[:, cols], in_=y[:, cols], func=ACT.Silu)
+                nc.sync.dma_start(out=out[P * d : P * (d + 1), cols], in_=o[:, cols])
+
+        bg_all = spread_row(0, "bg_all", 4)
+        gate_matmul(0)
+        ps_f = bank(5)
+        nc.tensor.matmul(out=ps_f[:, 0 : 2 * TILES], lhsT=rows[:, N : N + P], rhs=ident[:, 0 : 2 * TILES], start=True, stop=True)
+        node_f = keep.tile([P, 2 * TILES], F32, name="node_f")
+        nc.scalar.copy(out=node_f[:], in_=ps_f[:, 0 : 2 * TILES])
+        gate(0)
+        gate_matmul(1)
+        h_matmul(0)
+        b_all = spread_row(1, "b_all", 6)
+
+        for j in range(TILES):
+            if j + 1 < TILES:
+                gate(j + 1)
+            if j + 2 < TILES:
+                gate_matmul(j + 2)
+            if j + 1 < TILES:
+                h_matmul(j + 1)
+            message(j)
+            if j == TILES - 1:
+                keep_part(j - 1)
+            if j != TILES - 2:
+                keep_part(j)
+            if j == 0:
+                load_scales(a_s, a_scales)
+            if 1 <= j <= MG:
+                a_w.append(load_words("a_w%d" % (j - 1), a_words[j - 1 : j]))
+            g, r = divmod(j - 5, PACK)
+            if g >= 0 and r < 2:
+                interleave(g, r * N // 2, (r + 1) * N // 2, False)
+            if g >= 0 and r == 2:
+                quantize(g)
+            g, r = divmod(j - 8, PACK)
+            if g >= 0 and r < 2:
+                mix(2 * r, g)
+                mix(2 * r + 1, g)
+        nc.scalar.activation(out=warm[:, 1:2], in_=rows[:, N + P : N + P + 1], func=ACT.Silu)
+        for d in range(4, 8):
+            mix(d, 0)
+            mix(d, 1)
+        for d in range(8):
+            mix(d, 2)
+        interleave(3, 0, 320, True)
+        interleave(3, 320, N, False)
+        quantize(3)
+        for d in range(8):
+            mix(d, 3)
+            finish(d)
+        for d in range(8, TILES):
+            for g in range(MG):
+                mix(d, g)
+            finish(d, 2 if d == TILES - 1 else 1)

@@ -19,10 +19,20 @@ ACT = mybir.ActivationFunctionType
 P = 128
 PACK = 4
 K_PASS = P * PACK
-KG = K // K_PASS
-MG = M // K_PASS
+FEATURE_PASSES = K // K_PASS
+GROUPS = M // K_PASS
 TILES = M // P
 BANKS = 8
+X_EDGES = (0, 4, 8, 16)
+GATE_AHEAD = 2
+COPY_AHEAD = 4
+FIRST_SHARED = 5
+INTERLEAVE_LAG = 5
+VECTOR_CHANNELS = 320
+
+
+def shared(j):
+    return j >= FIRST_SHARED and j % 2 == 1 and j < TILES
 
 
 def tile_send_keep_graph_convolution_f2_kernel(
@@ -36,10 +46,10 @@ def tile_send_keep_graph_convolution_f2_kernel(
         ctx.enter_context(tc.manual_schedule())
 
         def bank(i):
-            return psum.tile([P, N], F32, name="bank%d" % i, tag="bank%d" % i)
+            return psum.tile([P, N], F32, name="bank%d" % i)
 
-        def plane(name, groups, width):
-            t = keep.tile([P, groups, width], U8, name=name, align_bytes=64)
+        def scale_tile(name, passes, width):
+            t = keep.tile([P, passes, width], U8, name=name, align_bytes=64)
             nc.vector.memset(t[:].bitcast(I32), 0)
             return t
 
@@ -51,185 +61,235 @@ def tile_send_keep_graph_convolution_f2_kernel(
                 )
 
         def load_words(name, words):
-            groups, width = words.shape[0], words.shape[2]
-            t = keep.tile([P, groups, width], U8, name=name, align_bytes=64)
+            t = keep.tile([P, words.shape[0], words.shape[2]], U8, name=name, align_bytes=64)
             nc.sync.dma_start(out=t[:].bitcast(I32), in_=words.bitcast(I32).rearrange("g p n -> p g n"))
             return t
 
-        rows = keep.tile([P, N + P + 16], BF16, name="rows")
-        nc.vector.memset(rows[:].bitcast(I32), 0)
-        wg_s = plane("wg_s", KG, N)
-        x_s = plane("x_s", KG, M)
-        wm_s = plane("wm_s", KG, N)
-        a_s = plane("a_s", MG, M)
+        def load_x(c):
+            return load_words("x_w%d" % c, x_words[:, :, 2 * P * X_EDGES[c] : 2 * P * X_EDGES[c + 1]])
+
+        bg_cols, b_cols = slice(0, N), slice(N, 2 * N)
+        src_cols, dst_cols = slice(2 * N, 2 * N + P), slice(2 * N + P, 2 * N + 2 * P)
+        zero_col = slice(2 * N + 2 * P, 2 * N + 2 * P + 1)
+        vectors = keep.tile([P, 2 * N + 2 * P + 2], BF16, name="vectors")
+        nc.vector.memset(vectors[:].bitcast(I32), 0)
+        ones = keep.tile([P, 2], BF16, name="ones")
+        nc.vector.memset(ones[:], 1.0)
+        wg_s = scale_tile("wg_s", FEATURE_PASSES, N)
+        x_s_first = scale_tile("x_s_first", FEATURE_PASSES, K_PASS)
+        wm_s = scale_tile("wm_s", FEATURE_PASSES, N)
+        x_s_rest = scale_tile("x_s_rest", FEATURE_PASSES, M - K_PASS)
+        a_s = scale_tile("a_s", GROUPS, M)
 
         warm = keep.tile([P, 2], F32, name="warm")
-        nc.scalar.activation(out=warm[:, 0:1], in_=rows[:, N + P : N + P + 1], func=ACT.Sigmoid)
-
+        nc.scalar.activation(out=warm[:, 0:1], in_=vectors[:, zero_col], func=ACT.Sigmoid)
         ident = keep.tile([P, P], BF16, name="ident")
         make_identity(nc, ident[:])
-        nc.gpsimd.dma_start(out=rows[0:TILES, N : N + P], in_=src.rearrange("(j p) -> j p", p=P))
-        nc.gpsimd.dma_start(out=rows[TILES : 2 * TILES, N : N + P], in_=dst.rearrange("(j p) -> j p", p=P))
 
-        def x_chunk(g):
-            return load_words("x_w%d" % g, x_words[:, :, 2 * K_PASS * g : 2 * K_PASS * (g + 1)])
-
+        x_w = [load_x(0)]
         wg_w = load_words("wg_w", wg_words)
-        x_w = [x_chunk(0)]
-        nc.sync.dma_start(out=rows[0:1, 0:N], in_=bg.unsqueeze(0))
+        nc.sync.dma_start(out=vectors[0:1, bg_cols], in_=bg.unsqueeze(0))
         load_scales(wg_s, wg_scales)
-        load_scales(x_s, x_scales)
-        load_scales(wm_s, wm_scales)
+        load_scales(x_s_first, x_scales[:, :, :K_PASS])
         wm_w = load_words("wm_w", wm_words)
-        nc.sync.dma_start(out=rows[1:2, 0:N], in_=b.unsqueeze(0))
-        for g in range(1, MG):
-            x_w.append(x_chunk(g))
+        load_scales(wm_s, wm_scales)
+        nc.sync.dma_start(out=vectors[0:TILES, src_cols], in_=src.rearrange("(j p) -> j p", p=P))
+        x_w.append(load_x(1))
+        nc.sync.dma_start(out=vectors[0:1, b_cols], in_=b.unsqueeze(0))
+        load_scales(x_s_rest, x_scales[:, :, K_PASS:])
+        nc.sync.dma_start(out=vectors[0:TILES, dst_cols], in_=dst.rearrange("(j p) -> j p", p=P))
         a_w = []
 
-        def spread_row(r, name, bank_id):
+        def on_all_partitions(name, cols, bank_id):
             ps = bank(bank_id)
-            nc.tensor.matmul(out=ps[:], lhsT=ident[:, r : r + 1].to_broadcast([P, P]), rhs=rows[:, 0:N], start=True, stop=True)
+            nc.tensor.matmul(
+                out=ps[:], lhsT=ones[:, 0:1].to_broadcast([P, P]), rhs=vectors[:, cols], start=True, stop=True
+            )
             t = keep.tile([P, N], F32, name=name)
             nc.scalar.copy(out=t[:], in_=ps[:])
             return t
 
+        def one_per_partition(name, cols, bank_id):
+            ps = bank(bank_id)
+            nc.tensor.matmul(
+                out=ps[:, 0 : 2 * TILES], lhsT=vectors[:, cols], rhs=ident[:, 0 : 2 * TILES], start=True, stop=True
+            )
+            t = keep.tile([P, TILES], F32, name=name)
+            nc.scalar.copy(out=t[:], in_=ps[:, 0:TILES])
+            return t
+
         def project(j, w, w_s, bank_id):
             ps = bank(bank_id)
-            g, jj = divmod(j, PACK)
-            for c in range(KG):
+            c = max(i for i in range(len(X_EDGES)) if X_EDGES[i] <= j)
+            w0 = 2 * P * (j - X_EDGES[c])
+            x_s, s0 = (x_s_first, P * j) if j < PACK else (x_s_rest, P * (j - PACK))
+            for f in range(FEATURE_PASSES):
                 nc.tensor.matmul_mx(
                     out=ps[:],
-                    lhsT=x_w[g][:, c, 2 * P * jj : 2 * P * (jj + 1)].bitcast(FP4X4),
-                    lhsT_scale=x_s[:, c, P * j : P * (j + 1)],
-                    rhs=w[:, c, :].bitcast(FP4X4),
-                    rhs_scale=w_s[:, c, :],
-                    start=(c == 0),
-                    stop=(c == KG - 1),
+                    lhsT=x_w[c][:, f, w0 : w0 + 2 * P].bitcast(FP4X4),
+                    lhsT_scale=x_s[:, f, s0 : s0 + P],
+                    rhs=w[:, f, :].bitcast(FP4X4),
+                    rhs_scale=w_s[:, f, :],
+                    start=(f == 0),
+                    stop=(f == FEATURE_PASSES - 1),
                 )
             return ps
 
-        gate_ps, h_ps, z, kept, v_rows, v_il, v_codes, v_scales, agg = {}, {}, {}, {}, {}, {}, {}, {}, {}
+        g_ps, h_ps, pre, z, kept, agg = {}, {}, {}, {}, {}, {}
+        v_rows, v_words, v_codes, v_scales = {}, {}, {}, {}
+        g_order = sorted(range(TILES), key=lambda j: j - (COPY_AHEAD if shared(j) else GATE_AHEAD))
 
-        def gate_matmul(j):
-            gate_ps[j] = project(j, wg_w, wg_s, j % 2)
+        def g_matmul(i):
+            if i < TILES:
+                g_ps[g_order[i]] = project(g_order[i], wg_w, wg_s, i % 2)
 
         def h_matmul(j):
-            h_ps[j] = project(j, wm_w, wm_s, 2 + j % 2)
+            h_ps[j] = project(j, wm_w, wm_s, 2 + j % 2 if j < TILES - 1 else 0)
+
+        def g_out(j):
+            pre[j] = work.tile([P, N], F32, name="pre", bufs=5)
+            if shared(j):
+                nc.scalar.copy(out=pre[j][:], in_=g_ps[j][:])
+            else:
+                nc.vector.tensor_tensor(out=pre[j][:], in0=g_ps[j][:], in1=bg_all[:], op=ALU.add)
+            g_matmul(g_order.index(j) + 2)
 
         def gate(j):
-            gb = work.tile([P, N], F32, name="gb")
-            nc.vector.tensor_tensor(out=gb[:], in0=gate_ps[j][:], in1=bg_all[:], op=ALU.add)
-            z[j] = work.tile([P, N], F32, name="z")
-            nc.scalar.activation(out=z[j][:], in_=gb[:], func=ACT.Sigmoid)
+            z[j] = work.tile([P, N], F32, name="z", bufs=5)
+            nc.scalar.activation(out=z[j][:], in_=pre[j][:], func=ACT.Sigmoid)
 
         def message(j):
-            v = work.tile([P, N], BF16, name="v", bufs=5)
-            nc.vector.scalar_tensor_tensor(
-                out=v[:], in0=h_ps[j][:], scalar=node_f[:, j : j + 1], in1=z[j][:], op0=ALU.mult, op1=ALU.mult
-            )
             g, jj = divmod(j, PACK)
+            v = work.tile([P, N], BF16, name="v", bufs=8)
+            nc.vector.scalar_tensor_tensor(
+                out=v[:], in0=h_ps[j][:], scalar=src_f[:, j : j + 1], in1=z[j][:], op0=ALU.mult, op1=ALU.mult
+            )
             if jj == 0:
-                v_rows[g] = work.tile([P, PACK, N], BF16, name="v_rows", bufs=2)
+                v_rows[g] = keep.tile([P, PACK, N], BF16, name="v_rows%d" % g)
             for t in range(PACK):
                 nc.sync.dma_start(out=v_rows[g][32 * jj : 32 * (jj + 1), t, :], in_=v[t:P:PACK, :])
 
-        def keep_part(j):
-            u = work.tile([P, N], F32, name="u")
-            nc.vector.scalar_tensor_tensor(
-                out=u[:], in0=z[j][:], scalar=1.0, in1=h_ps[j][:], op0=ALU.subtract, op1=ALU.mult
-            )
+        def keep_share(j):
             kept[j] = keep.tile([P, N], F32, name="kept%d" % j)
-            nc.gpsimd.tensor_tensor(out=kept[j][:], in0=b_all[:], in1=u[:], op=ALU.subtract)
+            nc.vector.scalar_tensor_tensor(
+                out=kept[j][:], in0=z[j][:], scalar=1.0, in1=h_ps[j][:], op0=ALU.subtract, op1=ALU.mult
+            )
 
-        def interleave(g, c0, c1, on_vector):
-            if g not in v_il:
-                v_il[g] = work.tile([P, N * PACK], BF16, name="v_il", bufs=2, align_bytes=64)
-            o = v_il[g][:, PACK * c0 : PACK * c1].rearrange("p (c i t) -> p c t i", i=4, t=PACK)
-            i = v_rows[g][:, :, c0:c1].rearrange("p t (c i) -> p c t i", i=4)
-            if on_vector:
-                nc.vector.tensor_copy(out=o, in_=i)
-            else:
-                nc.scalar.copy(out=o, in_=i)
+        def add_bias(j, target):
+            nc.gpsimd.tensor_tensor(out=target[:], in0=b_all[:], in1=kept[j][:], op=ALU.subtract)
+            kept[j] = target
+
+        def interleave(g, c0, c1, copy):
+            if c0 == 0:
+                last = g == GROUPS - 1
+                v_words[g] = work.tile(
+                    [P, N * PACK], BF16, name="v_last" if last else "v_words", bufs=1 if last else 2, align_bytes=64
+                )
+            copy(
+                out=v_words[g][:, PACK * c0 : PACK * c1].rearrange("p (c i t) -> p c t i", i=4, t=PACK),
+                in_=v_rows[g][:, :, c0:c1].rearrange("p t (c i) -> p c t i", i=4),
+            )
 
         def quantize(g):
             v_codes[g] = keep.tile([P, N], U32, name="v_codes%d" % g, align_bytes=64)
             v_scales[g] = keep.tile([P, N], U8, name="v_scales%d" % g, align_bytes=64)
-            nc.vector.quantize_mx(out=v_codes[g][:].bitcast(FP8X4), scales=v_scales[g][:], in_=v_il[g][:])
+            nc.vector.quantize_mx(out=v_codes[g][:].bitcast(FP8X4), scales=v_scales[g][:], in_=v_words[g][:])
 
-        def mix(d, g):
-            if g == 0:
-                agg[d] = bank((d + 4) % BANKS)
-            nc.tensor.matmul_mx(
-                out=agg[d][:],
-                lhsT=a_w[g][:, 0, 2 * P * d : 2 * P * (d + 1)].bitcast(FP4X4),
-                lhsT_scale=a_s[:, g, P * d : P * (d + 1)],
-                rhs=v_codes[g][:].bitcast(FP8X4),
-                rhs_scale=v_scales[g][:],
-                start=(g == 0),
-                stop=(g == MG - 1),
-            )
+        quantize_steps = [PACK * (g + 1) + INTERLEAVE_LAG for g in range(GROUPS - 2)]
+        plain_steps = [s for s in range(0, TILES, 2) if s + 1 not in quantize_steps]
+        early = list(range(len(plain_steps))) + quantize_steps
+        dests = early + [j for j in range(TILES) if j not in early]
+        dest_banks = (4, 5, 6, 7, 1, 3, 2, 0)
+        passes_done = [0] * TILES
 
-        def finish(d, parts=1):
+        def mix(d, upto):
+            j = dests[d]
+            for g in range(passes_done[d], upto):
+                if g == 0:
+                    agg[d] = bank(dest_banks[d % BANKS])
+                nc.tensor.matmul_mx(
+                    out=agg[d][:],
+                    lhsT=a_w[g][:, 0, 2 * P * j : 2 * P * (j + 1)].bitcast(FP4X4),
+                    lhsT_scale=a_s[:, g, P * j : P * (j + 1)],
+                    rhs=v_codes[g][:].bitcast(FP8X4),
+                    rhs_scale=v_scales[g][:],
+                    start=(g == 0),
+                    stop=(g == GROUPS - 1),
+                )
+            passes_done[d] = upto
+
+        def finish(d, parts):
+            j = dests[d]
             y = work.tile([P, N], F32, name="y")
             o = work.tile([P, N], F32, name="o", bufs=6)
             for h in range(parts):
                 cols = slice(h * N // parts, (h + 1) * N // parts)
                 nc.vector.scalar_tensor_tensor(
-                    out=y[:, cols], in0=agg[d][:, cols], scalar=node_f[:, TILES + d : TILES + d + 1],
-                    in1=kept[d][:, cols], op0=ALU.mult, op1=ALU.add,
+                    out=y[:, cols], in0=agg[d][:, cols], scalar=dst_f[:, j : j + 1], in1=kept[j][:, cols],
+                    op0=ALU.mult, op1=ALU.add,
                 )
                 nc.scalar.activation(out=o[:, cols], in_=y[:, cols], func=ACT.Silu)
-                nc.sync.dma_start(out=out[P * d : P * (d + 1), cols], in_=o[:, cols])
+                nc.sync.dma_start(out=out[P * j : P * (j + 1), cols], in_=o[:, cols])
 
-        bg_all = spread_row(0, "bg_all", 4)
-        gate_matmul(0)
-        ps_f = bank(5)
-        nc.tensor.matmul(out=ps_f[:, 0 : 2 * TILES], lhsT=rows[:, N : N + P], rhs=ident[:, 0 : 2 * TILES], start=True, stop=True)
-        node_f = keep.tile([P, 2 * TILES], F32, name="node_f")
-        nc.scalar.copy(out=node_f[:], in_=ps_f[:, 0 : 2 * TILES])
-        gate(0)
-        gate_matmul(1)
-        h_matmul(0)
-        b_all = spread_row(1, "b_all", 6)
-
-        for j in range(TILES):
-            if j + 1 < TILES:
-                gate(j + 1)
-            if j + 2 < TILES:
-                gate_matmul(j + 2)
-            if j + 1 < TILES:
-                h_matmul(j + 1)
-            message(j)
-            if j == TILES - 1:
-                keep_part(j - 1)
-            if j != TILES - 2:
-                keep_part(j)
-            if j == 0:
+        bg_all = on_all_partitions("bg_all", bg_cols, 4)
+        g_matmul(0)
+        g_matmul(1)
+        for s in range(-GATE_AHEAD, TILES):
+            if 1 <= s + 1 < TILES:
+                h_matmul(s + 1)
+            ahead = s + GATE_AHEAD
+            if ahead < TILES and not shared(ahead):
+                g_out(ahead)
+            if shared(s + COPY_AHEAD):
+                g_out(s + COPY_AHEAD)
+            if ahead < TILES:
+                gate(ahead)
+            if shared(ahead + 1):
+                nc.gpsimd.tensor_tensor(out=pre[ahead + 1][:], in0=pre[ahead + 1][:], in1=bg_all[:], op=ALU.add)
+            if s == -GATE_AHEAD:
+                h_matmul(0)
+                src_f = one_per_partition("src_f", src_cols, 5)
+            if s < 0:
+                continue
+            message(s)
+            if s in quantize_steps:
+                quantize(quantize_steps.index(s))
+            if s < TILES - 2:
+                keep_share(s)
+            if s == 0:
+                b_all = on_all_partitions("b_all", b_cols, 6)
+                x_w.append(load_x(2))
                 load_scales(a_s, a_scales)
-            if 1 <= j <= MG:
-                a_w.append(load_words("a_w%d" % (j - 1), a_words[j - 1 : j]))
-            g, r = divmod(j - 5, PACK)
-            if g >= 0 and r < 2:
-                interleave(g, r * N // 2, (r + 1) * N // 2, False)
-            if g >= 0 and r == 2:
-                quantize(g)
-            g, r = divmod(j - 8, PACK)
-            if g >= 0 and r < 2:
-                mix(2 * r, g)
-                mix(2 * r + 1, g)
-        nc.scalar.activation(out=warm[:, 1:2], in_=rows[:, N + P : N + P + 1], func=ACT.Silu)
-        for d in range(4, 8):
-            mix(d, 0)
-            mix(d, 1)
-        for d in range(8):
-            mix(d, 2)
-        interleave(3, 0, 320, True)
-        interleave(3, 320, N, False)
-        quantize(3)
-        for d in range(8):
-            mix(d, 3)
-            finish(d)
-        for d in range(8, TILES):
-            for g in range(MG):
-                mix(d, g)
+            if s == PACK:
+                dst_f = one_per_partition("dst_f", dst_cols, 7)
+            if s in quantize_steps:
+                add_bias(s, kept[s])
+            if s in plain_steps:
+                add_bias(plain_steps.index(s), kept[plain_steps.index(s)])
+            g, r = divmod(s - INTERLEAVE_LAG, PACK)
+            if 0 <= g < GROUPS - 2:
+                interleave(g, r * N // 4, (r + 1) * N // 4, nc.scalar.copy)
+            if g == GROUPS - 2 and r < 2:
+                interleave(g, r * N // 2, (r + 1) * N // 2, nc.scalar.copy)
+            if s >= INTERLEAVE_LAG and s % 2 == 1 and len(a_w) < GROUPS:
+                a_w.append(load_words("a_w%d" % len(a_w), a_words[len(a_w) : len(a_w) + 1]))
+            if s - 1 in quantize_steps:
+                for d in range(4 if s < TILES - 2 else 6):
+                    mix(d, quantize_steps.index(s - 1) + 1)
+        keep_share(TILES - 2)
+        keep_share(TILES - 1)
+        quantize(GROUPS - 2)
+        nc.scalar.activation(out=warm[:, 1:2], in_=vectors[:, zero_col], func=ACT.Silu)
+        for upto in (GROUPS - 2, GROUPS - 1):
+            for d in range(BANKS):
+                mix(d, upto)
+        interleave(GROUPS - 1, 0, VECTOR_CHANNELS, nc.vector.tensor_copy)
+        interleave(GROUPS - 1, VECTOR_CHANNELS, N, nc.scalar.copy)
+        quantize(GROUPS - 1)
+        first_late = work.tile([P, N], F32, name="v_last", bufs=1, align_bytes=64)
+        add_bias(dests[BANKS], first_late)
+        for j in dests[BANKS + 1 :]:
+            add_bias(j, kept[j])
+        for d in range(TILES):
+            mix(d, GROUPS)
             finish(d, 2 if d == TILES - 1 else 1)

from contextlib import ExitStack

import concourse.mybir as mybir
from concourse.masks import make_identity

M, K, N = 2048, 1024, 512
FLOPS = 2 * (2 * M * K * N) + 2 * M * M * N

F32 = mybir.dt.float32
BF16 = mybir.dt.bfloat16
I32 = mybir.dt.int32
U32 = mybir.dt.uint32
U8 = mybir.dt.uint8
FP4X4 = mybir.dt.float4_e2m1fn_x4
FP8X4 = mybir.dt.float8_e4m3fn_x4
ALU = mybir.AluOpType
ACT = mybir.ActivationFunctionType

P = 128
PACK = 4
K_PASS = P * PACK
FEATURE_PASSES = K // K_PASS
GROUPS = M // K_PASS
TILES = M // P
BANKS = 8
X_EDGES = (0, 4, 8, 16)
GATE_AHEAD = 2
COPY_AHEAD = 4
FIRST_SHARED = 5
INTERLEAVE_LAG = 5
VECTOR_CHANNELS = 320


def shared(j):
    return j >= FIRST_SHARED and j % 2 == 1 and j < TILES


def tile_send_keep_graph_convolution_f2_kernel(
    tc, x_words, x_scales, wm_words, wm_scales, wg_words, wg_scales, a_words, a_scales, bg, src, dst, b, out
):
    nc = tc.nc
    with ExitStack() as ctx:
        keep = ctx.enter_context(tc.tile_pool(name="keep", bufs=1))
        work = ctx.enter_context(tc.tile_pool(name="work", bufs=3))
        psum = ctx.enter_context(tc.psum_pool(name="psum", bufs=1))
        ctx.enter_context(tc.manual_schedule())

        def bank(i):
            return psum.tile([P, N], F32, name="bank%d" % i)

        def scale_tile(name, passes, width):
            t = keep.tile([P, passes, width], U8, name=name, align_bytes=64)
            nc.vector.memset(t[:].bitcast(I32), 0)
            return t

        def load_scales(t, scales):
            for q in range(4):
                nc.sync.dma_start(
                    out=t[32 * q : 32 * q + 4, :, :].bitcast(I32),
                    in_=scales.bitcast(I32)[:, 4 * q : 4 * q + 4, :].rearrange("g r n -> r g n"),
                )

        def load_words(name, words):
            t = keep.tile([P, words.shape[0], words.shape[2]], U8, name=name, align_bytes=64)
            nc.sync.dma_start(out=t[:].bitcast(I32), in_=words.bitcast(I32).rearrange("g p n -> p g n"))
            return t

        def load_x(c):
            return load_words("x_w%d" % c, x_words[:, :, 2 * P * X_EDGES[c] : 2 * P * X_EDGES[c + 1]])

        bg_cols, b_cols = slice(0, N), slice(N, 2 * N)
        src_cols, dst_cols = slice(2 * N, 2 * N + P), slice(2 * N + P, 2 * N + 2 * P)
        zero_col = slice(2 * N + 2 * P, 2 * N + 2 * P + 1)
        vectors = keep.tile([P, 2 * N + 2 * P + 2], BF16, name="vectors")
        nc.vector.memset(vectors[:].bitcast(I32), 0)
        ones = keep.tile([P, 2], BF16, name="ones")
        nc.vector.memset(ones[:], 1.0)
        wg_s = scale_tile("wg_s", FEATURE_PASSES, N)
        x_s_first = scale_tile("x_s_first", FEATURE_PASSES, K_PASS)
        wm_s = scale_tile("wm_s", FEATURE_PASSES, N)
        x_s_rest = scale_tile("x_s_rest", FEATURE_PASSES, M - K_PASS)
        a_s = scale_tile("a_s", GROUPS, M)

        warm = keep.tile([P, 2], F32, name="warm")
        nc.scalar.activation(out=warm[:, 0:1], in_=vectors[:, zero_col], func=ACT.Sigmoid)
        ident = keep.tile([P, P], BF16, name="ident")
        make_identity(nc, ident[:])

        x_w = [load_x(0)]
        wg_w = load_words("wg_w", wg_words)
        nc.sync.dma_start(out=vectors[0:1, bg_cols], in_=bg.unsqueeze(0))
        load_scales(wg_s, wg_scales)
        load_scales(x_s_first, x_scales[:, :, :K_PASS])
        wm_w = load_words("wm_w", wm_words)
        load_scales(wm_s, wm_scales)
        nc.sync.dma_start(out=vectors[0:TILES, src_cols], in_=src.rearrange("(j p) -> j p", p=P))
        x_w.append(load_x(1))
        nc.sync.dma_start(out=vectors[0:1, b_cols], in_=b.unsqueeze(0))
        load_scales(x_s_rest, x_scales[:, :, K_PASS:])
        nc.sync.dma_start(out=vectors[0:TILES, dst_cols], in_=dst.rearrange("(j p) -> j p", p=P))
        a_w = []

        def on_all_partitions(name, cols, bank_id):
            ps = bank(bank_id)
            nc.tensor.matmul(
                out=ps[:], lhsT=ones[:, 0:1].to_broadcast([P, P]), rhs=vectors[:, cols], start=True, stop=True
            )
            t = keep.tile([P, N], F32, name=name)
            nc.scalar.copy(out=t[:], in_=ps[:])
            return t

        def one_per_partition(name, cols, bank_id):
            ps = bank(bank_id)
            nc.tensor.matmul(
                out=ps[:, 0 : 2 * TILES], lhsT=vectors[:, cols], rhs=ident[:, 0 : 2 * TILES], start=True, stop=True
            )
            t = keep.tile([P, TILES], F32, name=name)
            nc.scalar.copy(out=t[:], in_=ps[:, 0:TILES])
            return t

        def project(j, w, w_s, bank_id):
            ps = bank(bank_id)
            c = max(i for i in range(len(X_EDGES)) if X_EDGES[i] <= j)
            w0 = 2 * P * (j - X_EDGES[c])
            x_s, s0 = (x_s_first, P * j) if j < PACK else (x_s_rest, P * (j - PACK))
            for f in range(FEATURE_PASSES):
                nc.tensor.matmul_mx(
                    out=ps[:],
                    lhsT=x_w[c][:, f, w0 : w0 + 2 * P].bitcast(FP4X4),
                    lhsT_scale=x_s[:, f, s0 : s0 + P],
                    rhs=w[:, f, :].bitcast(FP4X4),
                    rhs_scale=w_s[:, f, :],
                    start=(f == 0),
                    stop=(f == FEATURE_PASSES - 1),
                )
            return ps

        g_ps, h_ps, pre, z, kept, agg = {}, {}, {}, {}, {}, {}
        v_rows, v_words, v_codes, v_scales = {}, {}, {}, {}
        g_order = sorted(range(TILES), key=lambda j: j - (COPY_AHEAD if shared(j) else GATE_AHEAD))

        def g_matmul(i):
            if i < TILES:
                g_ps[g_order[i]] = project(g_order[i], wg_w, wg_s, i % 2)

        def h_matmul(j):
            h_ps[j] = project(j, wm_w, wm_s, 2 + j % 2 if j < TILES - 1 else 0)

        def g_out(j):
            pre[j] = work.tile([P, N], F32, name="pre", bufs=5)
            if shared(j):
                nc.scalar.copy(out=pre[j][:], in_=g_ps[j][:])
            else:
                nc.vector.tensor_tensor(out=pre[j][:], in0=g_ps[j][:], in1=bg_all[:], op=ALU.add)
            g_matmul(g_order.index(j) + 2)

        def gate(j):
            z[j] = work.tile([P, N], F32, name="z", bufs=5)
            nc.scalar.activation(out=z[j][:], in_=pre[j][:], func=ACT.Sigmoid)

        def message(j):
            g, jj = divmod(j, PACK)
            v = work.tile([P, N], BF16, name="v", bufs=8)
            nc.vector.scalar_tensor_tensor(
                out=v[:], in0=h_ps[j][:], scalar=src_f[:, j : j + 1], in1=z[j][:], op0=ALU.mult, op1=ALU.mult
            )
            if jj == 0:
                v_rows[g] = keep.tile([P, PACK, N], BF16, name="v_rows%d" % g)
            for t in range(PACK):
                nc.sync.dma_start(out=v_rows[g][32 * jj : 32 * (jj + 1), t, :], in_=v[t:P:PACK, :])

        def keep_share(j):
            kept[j] = keep.tile([P, N], F32, name="kept%d" % j)
            nc.vector.scalar_tensor_tensor(
                out=kept[j][:], in0=z[j][:], scalar=1.0, in1=h_ps[j][:], op0=ALU.subtract, op1=ALU.mult
            )

        def add_bias(j, target):
            nc.gpsimd.tensor_tensor(out=target[:], in0=b_all[:], in1=kept[j][:], op=ALU.subtract)
            kept[j] = target

        def interleave(g, c0, c1, copy):
            if c0 == 0:
                last = g == GROUPS - 1
                v_words[g] = work.tile(
                    [P, N * PACK], BF16, name="v_last" if last else "v_words", bufs=1 if last else 2, align_bytes=64
                )
            copy(
                out=v_words[g][:, PACK * c0 : PACK * c1].rearrange("p (c i t) -> p c t i", i=4, t=PACK),
                in_=v_rows[g][:, :, c0:c1].rearrange("p t (c i) -> p c t i", i=4),
            )

        def quantize(g):
            v_codes[g] = keep.tile([P, N], U32, name="v_codes%d" % g, align_bytes=64)
            v_scales[g] = keep.tile([P, N], U8, name="v_scales%d" % g, align_bytes=64)
            nc.vector.quantize_mx(out=v_codes[g][:].bitcast(FP8X4), scales=v_scales[g][:], in_=v_words[g][:])

        quantize_steps = [PACK * (g + 1) + INTERLEAVE_LAG for g in range(GROUPS - 2)]
        plain_steps = [s for s in range(0, TILES, 2) if s + 1 not in quantize_steps]
        early = list(range(len(plain_steps))) + quantize_steps
        dests = early + [j for j in range(TILES) if j not in early]
        dest_banks = (4, 5, 6, 7, 1, 3, 2, 0)
        passes_done = [0] * TILES

        def mix(d, upto):
            j = dests[d]
            for g in range(passes_done[d], upto):
                if g == 0:
                    agg[d] = bank(dest_banks[d % BANKS])
                nc.tensor.matmul_mx(
                    out=agg[d][:],
                    lhsT=a_w[g][:, 0, 2 * P * j : 2 * P * (j + 1)].bitcast(FP4X4),
                    lhsT_scale=a_s[:, g, P * j : P * (j + 1)],
                    rhs=v_codes[g][:].bitcast(FP8X4),
                    rhs_scale=v_scales[g][:],
                    start=(g == 0),
                    stop=(g == GROUPS - 1),
                )
            passes_done[d] = upto

        def finish(d, parts):
            j = dests[d]
            y = work.tile([P, N], F32, name="y")
            o = work.tile([P, N], F32, name="o", bufs=6)
            for h in range(parts):
                cols = slice(h * N // parts, (h + 1) * N // parts)
                nc.vector.scalar_tensor_tensor(
                    out=y[:, cols], in0=agg[d][:, cols], scalar=dst_f[:, j : j + 1], in1=kept[j][:, cols],
                    op0=ALU.mult, op1=ALU.add,
                )
                nc.scalar.activation(out=o[:, cols], in_=y[:, cols], func=ACT.Silu)
                nc.sync.dma_start(out=out[P * j : P * (j + 1), cols], in_=o[:, cols])

        bg_all = on_all_partitions("bg_all", bg_cols, 4)
        g_matmul(0)
        g_matmul(1)
        for s in range(-GATE_AHEAD, TILES):
            if 1 <= s + 1 < TILES:
                h_matmul(s + 1)
            ahead = s + GATE_AHEAD
            if ahead < TILES and not shared(ahead):
                g_out(ahead)
            if shared(s + COPY_AHEAD):
                g_out(s + COPY_AHEAD)
            if ahead < TILES:
                gate(ahead)
            if shared(ahead + 1):
                nc.gpsimd.tensor_tensor(out=pre[ahead + 1][:], in0=pre[ahead + 1][:], in1=bg_all[:], op=ALU.add)
            if s == -GATE_AHEAD:
                h_matmul(0)
                src_f = one_per_partition("src_f", src_cols, 5)
            if s < 0:
                continue
            message(s)
            if s in quantize_steps:
                quantize(quantize_steps.index(s))
            if s < TILES - 2:
                keep_share(s)
            if s == 0:
                b_all = on_all_partitions("b_all", b_cols, 6)
                x_w.append(load_x(2))
                load_scales(a_s, a_scales)
            if s == PACK:
                dst_f = one_per_partition("dst_f", dst_cols, 7)
            if s in quantize_steps:
                add_bias(s, kept[s])
            if s in plain_steps:
                add_bias(plain_steps.index(s), kept[plain_steps.index(s)])
            g, r = divmod(s - INTERLEAVE_LAG, PACK)
            if 0 <= g < GROUPS - 2:
                interleave(g, r * N // 4, (r + 1) * N // 4, nc.scalar.copy)
            if g == GROUPS - 2 and r < 2:
                interleave(g, r * N // 2, (r + 1) * N // 2, nc.scalar.copy)
            if s >= INTERLEAVE_LAG and s % 2 == 1 and len(a_w) < GROUPS:
                a_w.append(load_words("a_w%d" % len(a_w), a_words[len(a_w) : len(a_w) + 1]))
            if s - 1 in quantize_steps:
                for d in range(4 if s < TILES - 2 else 6):
                    mix(d, quantize_steps.index(s - 1) + 1)
        keep_share(TILES - 2)
        keep_share(TILES - 1)
        quantize(GROUPS - 2)
        nc.scalar.activation(out=warm[:, 1:2], in_=vectors[:, zero_col], func=ACT.Silu)
        for upto in (GROUPS - 2, GROUPS - 1):
            for d in range(BANKS):
                mix(d, upto)
        interleave(GROUPS - 1, 0, VECTOR_CHANNELS, nc.vector.tensor_copy)
        interleave(GROUPS - 1, VECTOR_CHANNELS, N, nc.scalar.copy)
        quantize(GROUPS - 1)
        first_late = work.tile([P, N], F32, name="v_last", bufs=1, align_bytes=64)
        add_bias(dests[BANKS], first_late)
        for j in dests[BANKS + 1 :]:
            add_bias(j, kept[j])
        for d in range(TILES):
            mix(d, GROUPS)
            finish(d, 2 if d == TILES - 1 else 1)
